import numpy as np
import ml_dtypes


def mxq(x, axis, fmt="e4m3"):
    dtype, down = {"e4m3": (ml_dtypes.float8_e4m3fn, 7), "e5m2": (ml_dtypes.float8_e5m2, 14)}[fmt]
    v = np.moveaxis(np.asarray(x, np.float32).astype(ml_dtypes.bfloat16).astype(np.float64), axis, -1)
    blocks = v.reshape(v.shape[:-1] + (-1, 32))
    amax = np.abs(blocks).max(-1, keepdims=True)
    byte = np.maximum(np.where(amax > 0, np.frexp(amax)[1] - 1 + 127, 0) - down, 1)
    scale = np.exp2(byte - 127.0)
    codes = (blocks / scale).astype(np.float32).astype(dtype).astype(np.float64)
    return np.moveaxis((codes * scale).reshape(v.shape), -1, axis)


WIDE = False


def mx_kscale(k):
    if not WIDE:
        return np.ones(k)
    levels = np.array([10, -10, 5, -5, 0])
    if k % 512:
        return np.exp2(np.random.permutation(np.resize(levels, k // 32))).repeat(32)
    a = np.empty((k // 512, 16))
    for p in range(k // 512):
        a[p, :8] = np.random.permutation(np.resize(levels, 8))
        for g in range(8):
            far = levels[np.abs(levels - a[p, g]) >= 10]
            a[p, g + 8] = far[np.random.randint(len(far))]
    return np.exp2(a.ravel()).repeat(32)


def f64(x):
    return np.asarray(x).astype(np.float64)


def striped(idx):
    return np.tile(idx.reshape(-1, 16).T, (8, 1)).astype(np.uint16)


def unstriped(offs):
    return offs[:16].T.reshape(-1).astype(np.int64)


E2M1 = np.array([0.0, 0.5, 1.0, 1.5, 2.0, 3.0, 4.0, 6.0, -0.0, -0.5, -1.0, -1.5, -2.0, -3.0, -4.0, -6.0])


def pack_weight(w, fmt):
    k, n = w.shape
    w = f64(np.asarray(w, np.float32).astype(ml_dtypes.bfloat16)).reshape(k // 32, 32, n)
    amax = np.abs(w).max(1)
    if fmt == "e4m3":
        byte = np.frexp(amax)[1] - 1 + 127 - 7
    else:
        mant, ex = np.frexp(amax / 6.0)
        byte = np.where(mant > 0.5, ex, ex - 1) + 127
    byte = np.clip(np.where(amax > 0, byte, 1), 1, 254)
    scaled = (w * np.exp2(127.0 - byte)[:, None, :]).reshape(k, n).astype(np.float32)
    by_word = np.ascontiguousarray(scaled.reshape(k // 512, 128, 4, n).transpose(0, 1, 3, 2))
    if fmt == "e4m3":
        words = by_word.astype(ml_dtypes.float8_e4m3fn).view(np.uint8)
    else:
        c = by_word.astype(ml_dtypes.float4_e2m1fn).view(np.uint8) & 0xF
        words = (c[..., 0::2] | (c[..., 1::2] << 4)).reshape(k // 512, 128, 2 * n)
    return np.ascontiguousarray(words), np.ascontiguousarray(byte.astype(np.uint8).reshape(k // 512, 16, n))


def unpack_weight(words, scales, fmt):
    g, _, n = scales.shape
    words = np.ascontiguousarray(words).reshape(g, 128, n, -1)
    if fmt == "e4m3":
        vals = words.view(ml_dtypes.float8_e4m3fn).astype(np.float64)
    else:
        nib = np.empty((g, 128, n, 4), np.uint8)
        nib[..., 0::2] = words & 0xF
        nib[..., 1::2] = words >> 4
        vals = E2M1[nib]
    vals = vals * np.repeat(np.exp2(scales.astype(np.float64) - 127.0), 8, axis=1)[..., None]
    return vals.transpose(0, 1, 3, 2).reshape(g * 512, n)


def gelu(v):
    return 0.5 * v * (1.0 + np.tanh(np.sqrt(2.0 / np.pi) * (v + 0.044715 * v**3)))


K, T, E, C, H, N = 1024, 1024, 6, 128, 512, 256
R = 4


def by_expert(wq, xq):
    return np.concatenate([wq[e].T @ xq[:, e * C:(e + 1) * C] for e in range(E)], axis=1)


def setup_inputs():
    n = np.random.standard_normal
    s = mx_kscale(K)[:, None]
    u = mx_kscale(H)
    slot_token = np.concatenate([r * (T // R) + np.random.permutation(T // R)[:C // R] for e in range(E) for r in range(R)])
    w1 = [pack_weight(m, "e2m1") for m in n((E, K, H)) / np.sqrt(K) / s[None]]
    w3 = [pack_weight(m, "e2m1") for m in n((E, K, H)) / np.sqrt(K) / s[None] * u[None, None, :]]
    w2 = [pack_weight(m, "e2m1") for m in n((E, H, N)) / np.sqrt(H) / u[None, :, None]]
    return {
        "xT": (n((K, T)) * s).astype(np.float32),
        "w1_words": np.stack([m[0] for m in w1]),
        "w1_scales": np.stack([m[1] for m in w1]),
        "w3_words": np.stack([m[0] for m in w3]),
        "w3_scales": np.stack([m[1] for m in w3]),
        "w2_words": np.stack([m[0] for m in w2]),
        "w2_scales": np.stack([m[1] for m in w2]),
        "offs": striped(slot_token),
    }


def reference(xT, w1_words, w1_scales, w3_words, w3_scales, w2_words, w2_scales, offs):
    idx = unstriped(offs)
    w1 = np.stack([unpack_weight(w1_words[e], w1_scales[e], "e2m1") for e in range(E)])
    w3 = np.stack([unpack_weight(w3_words[e], w3_scales[e], "e2m1") for e in range(E)])
    w2 = np.stack([unpack_weight(w2_words[e], w2_scales[e], "e2m1") for e in range(E)])
    xq = mxq(f64(xT)[:, idx], 0, "e4m3")
    h = gelu(by_expert(w1, xq))
    h = h * by_expert(w3, xq)
    y = by_expert(w2, mxq(h, 0, "e4m3"))
    return y.reshape(N, E, R, C // R).transpose(0, 2, 1, 3).reshape(N, E * C)

from contextlib import ExitStack

import concourse.mybir as mybir
from concourse.masks import make_identity

K, T, E, C, H, N = 1024, 1024, 6, 128, 512, 256
R = 4
S = E * C
P = 128
PASSES = K // 512
RU = C // R

F32 = mybir.dt.float32
BF16 = mybir.dt.bfloat16
I32 = mybir.dt.int32
U32 = mybir.dt.uint32
U16 = mybir.dt.uint16
U8 = mybir.dt.uint8
FP8X4 = mybir.dt.float8_e4m3fn_x4
FP4X4 = mybir.dt.float4_e2m1fn_x4
ACT = mybir.ActivationFunctionType
MULT = mybir.AluOpType.mult

FLOPS = 2 * S * (2 * K * H + H * N)

CHUNK = 512
V_TOKENS = {(0, 0): 192, (0, 1): 192, (1, 0): 192, (1, 1): 320}
GATHER = 384
FIRST = 4


def tile_moe_eps_glu_gelu_kernel(
    tc, xT, w1_words, w1_scales, w3_words, w3_scales, w2_words, w2_scales, offs, out
):
    nc = tc.nc
    with ExitStack() as ctx:
        keep = ctx.enter_context(tc.tile_pool(name="keep", bufs=1))
        ring = ctx.enter_context(tc.tile_pool(name="ring", bufs=2))
        psum = ctx.enter_context(tc.psum_pool(name="psum", bufs=2))

        offsets = keep.tile([P, S // 16], U16, name="offsets")

        s1 = keep.tile([P, E * PASSES, H], U8, name="s1", align_bytes=64)
        s3 = keep.tile([P, E * PASSES, H], U8, name="s3", align_bytes=64)
        s2 = keep.tile([P, E, N], U8, name="s2", align_bytes=64)
        tb = [keep.tile([P, T], U8, name=f"tb{s}", align_bytes=64) for s in range(PASSES)]
        zero = keep.tile([P, 1], F32, name="zero")
        warm = keep.tile([P, 1], F32, name="warm")
        nc.vector.memset(zero[:], 0.0)
        for t in (s1, s3, s2):
            nc.vector.memset(t[:].rearrange("p a b -> p (a b)").bitcast(I32), 0)
        for t in tb:
            nc.vector.memset(t[:].bitcast(I32), 0)
        nc.scalar.activation(out=warm[:], in_=zero[:], func=ACT.Gelu_apprx_tanh)
        ident = keep.tile([P, P], F32, name="ident")
        make_identity(nc, ident[:])

        raw = {}
        for s in range(PASSES):
            for c in range(T // CHUNK):
                raw[s, c] = keep.tile([P, 4, CHUNK], F32, name=f"raw{s}{c}")
                nc.sync.dma_start(
                    out=raw[s, c][:],
                    in_=xT[512 * s : 512 * (s + 1), CHUNK * c : CHUNK * (c + 1)].rearrange("(p j) w -> p j w", j=4),
                )
                if (s, c) == (0, 0):
                    nc.sync.dma_start(offsets[:], offs)
        for dst, src in ((s1, w1_scales), (s3, w3_scales), (s2, w2_scales)):
            rows = src.bitcast(I32).rearrange("e s (q r) i -> r q (e s) i", r=4)
            for r in range(4):
                nc.sync.dma_start(out=dst[:].bitcast(I32)[r:P:32], in_=rows[r])
        w1 = [keep.tile([P, PASSES, 2 * H], U8, name=f"w1_{e}", align_bytes=64) for e in range(E)]
        w3 = [keep.tile([P, PASSES, 2 * H], U8, name=f"w3_{e}", align_bytes=64) for e in range(E)]
        w2 = [keep.tile([P, E // 2, 2 * N], U8, name=f"w2_{g}", align_bytes=64) for g in range(2)]
        for e in range(E):
            for dst, src in ((w1, w1_words), (w3, w3_words)):
                nc.sync.dma_start(
                    out=dst[e][:].bitcast(I32), in_=src[e].bitcast(I32).rearrange("s p b -> p s b")
                )
            if e in (0, 3):
                g = e // 3
                nc.sync.dma_start(
                    out=w2[g][:].bitcast(I32),
                    in_=w2_words[3 * g : 3 * g + 3].bitcast(I32).rearrange("e s p b -> p (e s) b"),
                )

        gw = [keep.tile([P, S], U32, name=f"gw{s}", align_bytes=64) for s in range(PASSES)]
        gb = [keep.tile([P, S], U8, name=f"gb{s}", align_bytes=64) for s in range(PASSES)]
        for s in range(PASSES):
            tw = keep.tile([P, T], U32, name=f"tw{s}", align_bytes=64)
            for c in range(T // CHUNK):
                grouped = keep.tile([P, CHUNK, 4], BF16, name=f"grouped{s}{c}", align_bytes=64)
                src = raw[s, c][:].rearrange("p j w -> p w j")
                v = V_TOKENS[s, c]
                nc.vector.tensor_copy(out=grouped[:, :v, :], in_=src[:, :v, :])
                nc.scalar.activation(out=grouped[:, v:, :], in_=src[:, v:, :], func=ACT.Copy)
                nc.vector.quantize_mx(
                    out=tw[:, CHUNK * c : CHUNK * (c + 1)].bitcast(FP8X4),
                    scales=tb[s][:, CHUNK * c : CHUNK * (c + 1)],
                    in_=grouped[:].rearrange("p w j -> p (w j)"),
                )
            for g0 in range(0, S, GATHER):
                idx = offsets[:, g0 // 16 : (g0 + GATHER) // 16]
                nc.vector.tensor_copy(gw[s][:, g0 : g0 + GATHER], tw[:].indirect(idx))
                nc.vector.tensor_copy(gb[s][:, g0 : g0 + GATHER], tb[s][:].indirect(idx))

        ysb = [
            keep.tile([P, N // P, R, FIRST * RU], F32, name="ysb0"),
            keep.tile([P, N // P, R, (E - FIRST) * RU], F32, name="ysb1"),
        ]
        banks = {}
        hs = {}

        def first_layer(e):
            cols = slice(e * C, (e + 1) * C)
            pa = psum.tile([P, H], F32, name="pa")
            pb = psum.tile([P, H], F32, name="pb")
            for bank, words, scales in ((pa, w1, s1), (pb, w3, s3)):
                for s in range(PASSES):
                    nc.tensor.matmul_mx(
                        out=bank[:],
                        lhsT=gw[s][:, cols].bitcast(FP8X4),
                        lhsT_scale=gb[s][:, cols],
                        rhs=words[e][:, s, :].bitcast(FP4X4),
                        rhs_scale=scales[:, PASSES * e + s, :],
                        start=(s == 0),
                        stop=(s == PASSES - 1),
                    )
            g = ring.tile([P, H], F32, name="g")
            nc.scalar.activation(out=g[:], in_=pa[:], func=ACT.Gelu_apprx_tanh)
            h = ring.tile([P, H], BF16, name="h")
            nc.vector.tensor_tensor(
                h[:].rearrange("p (u q d) -> p u q d", u=2, d=2),
                pb[:].rearrange("p (q u d) -> p u q d", u=2, d=2),
                g[:].rearrange("p (q u d) -> p u q d", u=2, d=2),
                MULT,
            )
            banks[e] = h

        def turn(e):
            h = banks[e]
            tr = psum.tile([P, 4, P], F32, name="tr")
            for u in range(2):
                nc.tensor.transpose(tr[:, u, :], h[:].bitcast(F32)[:, P * u : P * (u + 1)], ident[:])
            hg = ring.tile([P, C, 4], BF16, name="hg", align_bytes=64)
            nc.scalar.copy(out=hg[:].bitcast(F32), in_=tr[:, 0:2, :].rearrange("p u r -> p r u"))
            hq = ring.tile([P, C], U32, name="hq", align_bytes=64)
            hb = ring.tile([P, C], U8, name="hb", align_bytes=64)
            nc.vector.quantize_mx(
                out=hq[:].bitcast(FP8X4), scales=hb[:], in_=hg[:].rearrange("p c t -> p (c t)")
            )
            hs[e] = (hq, hb)

        def second_layer(e):
            hq, hb = hs[e]
            y = psum.tile([P, 4, P], F32, name="y")
            for t in range(N // P):
                nc.tensor.matmul_mx(
                    out=y[:, t, :],
                    lhsT=w2[e // 3][:, e % 3, 2 * P * t : 2 * P * (t + 1)].bitcast(FP4X4),
                    lhsT_scale=s2[:, e, P * t : P * (t + 1)],
                    rhs=hq[:].bitcast(FP8X4),
                    rhs_scale=hb[:],
                    start=True,
                    stop=True,
                )
            part = 0 if e < FIRST else 1
            u0 = RU * (e - FIRST * part)
            nc.scalar.copy(
                out=ysb[part][:, :, :, u0 : u0 + RU], in_=y[:, 0:2, :].rearrange("p t (m u) -> p t m u", m=R)
            )

        def store(part):
            lo = 0 if part == 0 else FIRST * RU
            hi = FIRST * RU if part == 0 else E * RU
            for t in range(N // P):
                nc.sync.dma_start(
                    out=out[P * t : P * (t + 1), :].rearrange("p (m x) -> p m x", m=R)[:, :, lo:hi],
                    in_=ysb[part][:, t],
                )

        for step in range(E + 2):
            if step < E:
                first_layer(step)
            if 1 <= step <= E:
                turn(step - 1)
            if step >= 2:
                second_layer(step - 2)
                if step - 2 == FIRST - 1:
                    store(0)
        store(1)
